import numpy as np
import ml_dtypes


def mxq(x, axis, fmt="e4m3"):
    dtype, down = {"e4m3": (ml_dtypes.float8_e4m3fn, 7), "e5m2": (ml_dtypes.float8_e5m2, 14)}[fmt]
    v = np.moveaxis(np.asarray(x, np.float32).astype(ml_dtypes.bfloat16).astype(np.float64), axis, -1)
    blocks = v.reshape(v.shape[:-1] + (-1, 32))
    amax = np.abs(blocks).max(-1, keepdims=True)
    byte = np.maximum(np.where(amax > 0, np.frexp(amax)[1] - 1 + 127, 0) - down, 1)
    scale = np.exp2(byte - 127.0)
    codes = (blocks / scale).astype(np.float32).astype(dtype).astype(np.float64)
    return np.moveaxis((codes * scale).reshape(v.shape), -1, axis)


WIDE = False


def mx_kscale(k):
    if not WIDE:
        return np.ones(k)
    levels = np.array([24, -24, 12, -12, 0])
    if k % 512:
        return np.exp2(np.random.permutation(np.resize(levels, k // 32))).repeat(32)
    a = np.empty((k // 512, 16))
    for p in range(k // 512):
        a[p, :8] = np.random.permutation(np.resize(levels, 8))
        for g in range(8):
            far = levels[np.abs(levels - a[p, g]) >= 10]
            a[p, g + 8] = far[np.random.randint(len(far))]
    return np.exp2(a.ravel()).repeat(32)


def f64(x):
    return np.asarray(x).astype(np.float64)


def striped8(idx):
    return np.concatenate([v.reshape(-1, 16).T for v in idx]).astype(np.uint16)


def unstriped8(offs):
    return np.stack([offs[16 * g:16 * g + 16].T.reshape(-1) for g in range(8)]).astype(np.int64)


E2M1 = np.array([0.0, 0.5, 1.0, 1.5, 2.0, 3.0, 4.0, 6.0, -0.0, -0.5, -1.0, -1.5, -2.0, -3.0, -4.0, -6.0])


def pack_weight(w, fmt):
    k, n = w.shape
    w = f64(np.asarray(w, np.float32).astype(ml_dtypes.bfloat16)).reshape(k // 32, 32, n)
    amax = np.abs(w).max(1)
    if fmt == "e4m3":
        byte = np.frexp(amax)[1] - 1 + 127 - 7
    else:
        mant, ex = np.frexp(amax / 6.0)
        byte = np.where(mant > 0.5, ex, ex - 1) + 127
    byte = np.clip(np.where(amax > 0, byte, 1), 1, 254)
    scaled = (w * np.exp2(127.0 - byte)[:, None, :]).reshape(k, n).astype(np.float32)
    by_word = np.ascontiguousarray(scaled.reshape(k // 512, 128, 4, n).transpose(0, 1, 3, 2))
    if fmt == "e4m3":
        words = by_word.astype(ml_dtypes.float8_e4m3fn).view(np.uint8)
    else:
        c = by_word.astype(ml_dtypes.float4_e2m1fn).view(np.uint8) & 0xF
        words = (c[..., 0::2] | (c[..., 1::2] << 4)).reshape(k // 512, 128, 2 * n)
    return np.ascontiguousarray(words), np.ascontiguousarray(byte.astype(np.uint8).reshape(k // 512, 16, n))


def unpack_weight(words, scales, fmt):
    g, _, n = scales.shape
    words = np.ascontiguousarray(words).reshape(g, 128, n, -1)
    if fmt == "e4m3":
        vals = words.view(ml_dtypes.float8_e4m3fn).astype(np.float64)
    else:
        nib = np.empty((g, 128, n, 4), np.uint8)
        nib[..., 0::2] = words & 0xF
        nib[..., 1::2] = words >> 4
        vals = E2M1[nib]
    vals = vals * np.repeat(np.exp2(scales.astype(np.float64) - 127.0), 8, axis=1)[..., None]
    return vals.transpose(0, 1, 3, 2).reshape(g * 512, n)


def planes(y):
    n, m = y.shape
    v = y.astype(np.float32).astype(ml_dtypes.bfloat16).astype(np.float64).reshape(n // 32, 32, m)
    top = np.abs(v).max(1)
    byte = np.clip(np.where(top > 0, np.frexp(top)[1] - 1 + 127 - 7, 1), 1, 254)
    codes = (v * np.exp2(127.0 - byte)[:, None, :]).reshape(n, m).astype(np.float32).astype(ml_dtypes.float8_e4m3fn).view(np.uint8)
    words = codes.reshape(n // 512, 128, 4, m).transpose(0, 1, 3, 2)
    return np.ascontiguousarray(words), np.ascontiguousarray(byte.astype(np.uint8).reshape(n // 512, 16, m))


K, R, N, T, J = 512, 512, 512, 2048, 1024


def setup_inputs():
    n = np.random.standard_normal
    s = mx_kscale(K)[:, None]
    u = mx_kscale(R)[:, None]
    p_wg = pack_weight(n((K, R)) / np.sqrt(K) / s, "e4m3")
    p_wu = pack_weight(n((K, R)) / np.sqrt(K) / s * u.T, "e4m3")
    return {
        "xT": (n((K, T)) * s).astype(np.float32),
        "wgt": np.repeat(np.random.uniform(0.5, 2.0, (8, J)), 16, axis=0).astype(np.float32),
        "wg_words": p_wg[0],
        "wg_scales": p_wg[1],
        "wu_words": p_wu[0],
        "wu_scales": p_wu[1],
        "wd": (n((R, N)) / np.sqrt(R) / u).astype(np.float32),
        "res": (n((N, J))).astype(np.float32),
        "offs": striped8(np.stack([np.random.permutation(T)[:J] for _ in range(8)])),
    }


def reference(xT, wgt, wg_words, wg_scales, wu_words, wu_scales, wd, res, offs):
    idx = unstriped8(offs)
    rows = np.arange(K)
    xg = f64(wgt)[rows // 4 % 128] * f64(xT)[rows[:, None], idx[rows % 512 // 64]]
    xT_ = mxq(xg, 0, "e4m3")
    wg_ = unpack_weight(wg_words, wg_scales, "e4m3")
    wu_ = unpack_weight(wu_words, wu_scales, "e4m3")
    ga = wg_.T @ xT_
    ub = wu_.T @ xT_
    h = np.tanh(ga) * ub
    h_ = mxq(h, 0, "e4m3")
    wd_ = mxq(f64(wd), 0, "e4m3")
    y = wd_.T @ h_
    out_0 = f64(res) + y
    return (out_0,) + planes(out_0)

@@ -1,0 +1,182 @@
+from contextlib import ExitStack
+
+import concourse.mybir as mybir
+
+K, R, N, T, J = 512, 512, 512, 2048, 1024
+FLOPS = 2 * J * (K * R * 2 + R * N)
+
+F32 = mybir.dt.float32
+BF16 = mybir.dt.bfloat16
+I32 = mybir.dt.int32
+U16 = mybir.dt.uint16
+U8 = mybir.dt.uint8
+FP8X4 = mybir.dt.float8_e4m3fn_x4
+MULT = mybir.AluOpType.mult
+ADD = mybir.AluOpType.add
+TANH = mybir.ActivationFunctionType.Tanh
+
+P = 128
+PACK = 4
+W = 128
+CHUNKS = J // W
+STORE = 256
+LEAD = 256
+
+
+def tile_list_tanh_resP_kernel(tc, xT, wgt, wg_words, wg_scales, wu_words, wu_scales, wd, res, offs, out_0, out_1, out_2):
+    nc = tc.nc
+    with ExitStack() as ctx:
+        keep = ctx.enter_context(tc.tile_pool(name="keep", bufs=1))
+        ring = ctx.enter_context(tc.tile_pool(name="ring", bufs=3))
+        psum = ctx.enter_context(tc.psum_pool(name="psum", bufs=1))
+
+        offsets = keep.tile([P, J // 16], U16, name="offsets")
+        nc.sync.dma_start(offsets[:], offs)
+
+        x_rows = xT.rearrange("(p i) t -> i p t", i=PACK)
+        planes = [keep.tile([P, T], F32, name=f"plane{i}") for i in range(PACK)]
+        wgt_lead = keep.tile([P, LEAD], F32, name="wgt_lead")
+        wgt_rest = keep.tile([P, J - LEAD], F32, name="wgt_rest")
+        nc.sync.dma_start(wgt_lead[:], wgt[:, :LEAD])
+        nc.sync.dma_start(planes[0][:], x_rows[0])
+        nc.sync.dma_start(wgt_rest[:], wgt[:, LEAD:])
+        for i in range(1, PACK):
+            nc.sync.dma_start(planes[i][:], x_rows[i])
+
+        raw_words = []
+        for name, words in (("wg_raw", wg_words), ("wu_raw", wu_words)):
+            raw = keep.tile([P, R], I32, name=name)
+            nc.sync.dma_start(raw[:], words[0].rearrange("p r i -> p (r i)").bitcast(I32))
+            raw_words.append(raw)
+        wd_raw = keep.tile([P, PACK, N], F32, name="wd_raw")
+        nc.sync.dma_start(wd_raw[:], wd.rearrange("(p i) n -> p i n", i=PACK))
+        res_rows = res.rearrange("(p t) j -> p t j", t=PACK)
+        res_sb = []
+        for s in range(J // STORE):
+            part = keep.tile([P, PACK, STORE], F32, name=f"res{s}")
+            nc.sync.dma_start(part[:], res_rows[:, :, s * STORE:(s + 1) * STORE])
+            res_sb.append(part)
+
+        scales_raw = keep.tile([P, R], U8, name="scales_raw")
+        nc.gpsimd.memset(scales_raw[:].bitcast(I32), 0)
+        for first, scales in ((0, wg_scales), (4, wu_scales)):
+            for q in range(4):
+                nc.gpsimd.dma_start(scales_raw[32 * q + first:32 * q + first + 4, :].bitcast(I32),
+                                    scales[0, 4 * q:4 * q + 4, :].bitcast(I32))
+
+        warm = keep.tile([P, 1], F32, name="warm")
+        nc.vector.memset(warm[:], 0.0)
+        nc.scalar.activation(warm[:], warm[:], TANH)
+
+        def wgt_cols(a, b):
+            return wgt_lead[:, a:b] if b <= LEAD else wgt_rest[:, a - LEAD:b - LEAD]
+
+        def gather(out, i, a, b):
+            nc.vector.tensor_tensor(out, planes[i][:].indirect(offsets[:, a // 16:b // 16]), wgt_cols(a, b), MULT)
+
+        g01 = keep.tile([P, 2, J], F32, name="g01")
+        for i in range(2):
+            gather(g01[:, i, :LEAD], i, 0, LEAD)
+            gather(g01[:, i, LEAD:], i, LEAD, J)
+        g23 = [keep.tile([P, 2, W], F32, name=f"g23_{c}") for c in range(CHUNKS)]
+        xb = [keep.tile([P, W, PACK], BF16, name=f"xb{c}", align_bytes=64) for c in range(CHUNKS)]
+
+        def weave(engine_copy, dst, src):
+            engine_copy(dst.rearrange("p (c i) t -> p c t i", i=4), src.rearrange("p t (c i) -> p c t i", i=4))
+
+        for c in range(CHUNKS):
+            weave(nc.scalar.copy, xb[c][:, :, 0:2], g01[:, :, c * W:(c + 1) * W])
+        for c in range(CHUNKS):
+            gather(g23[c][:, 0, :], 2, c * W, (c + 1) * W)
+
+        w1_words = [keep.tile([P, R], I32, name=f"w1_words{k}", align_bytes=64) for k in range(2)]
+        w1_scales = keep.tile([P, R], U8, name="w1_scales", align_bytes=64)
+        nc.vector.tensor_copy(w1_scales[:].rearrange("p (t c i) -> p c t i", t=4, i=16),
+                              scales_raw[:].rearrange("p (c i t) -> p c t i", t=4, i=16))
+
+        def deal_w1(k):
+            nc.vector.tensor_copy(w1_words[k][:].rearrange("p (t c i) -> p c t i", t=4, i=4),
+                                  raw_words[k][:].rearrange("p (c i t) -> p c t i", t=4, i=4))
+
+        wd_bf = keep.tile([P, N, PACK], BF16, name="wd_bf", align_bytes=64)
+        wd_words = keep.tile([P, N], I32, name="wd_words", align_bytes=64)
+        wd_scales = keep.tile([P, N], U8, name="wd_scales", align_bytes=64)
+
+        def deal_wd(k):
+            ms = slice(32 * k, 32 * (k + 1))
+            nc.scalar.copy(wd_bf[:].rearrange("p (t m) i -> p m i t", t=4)[:, ms],
+                           wd_raw[:].rearrange("p i (m t) -> p m i t", t=4)[:, ms])
+
+        def quantize(words, scales, src):
+            nc.vector.quantize_mx(out=words.bitcast(FP8X4), scales=scales, in_=src.rearrange("p j t -> p (j t)"))
+
+        def product(bank, words, scales, rhs, rhs_scale):
+            for t in range(PACK):
+                cols = slice(t * P, (t + 1) * P)
+                nc.tensor.matmul_mx(out=bank[:, t, :], lhsT=words[:, cols].bitcast(FP8X4), lhsT_scale=scales[:, cols],
+                                    rhs=rhs.bitcast(FP8X4), rhs_scale=rhs_scale, start=True, stop=True)
+
+        out_rows = out_0.rearrange("(p t) j -> p t j", t=PACK)
+        out_words = out_1[0].rearrange("p j i -> p (j i)").bitcast(I32)
+        o32 = [keep.tile([P, PACK, STORE], F32, name=f"o32_{s}") for s in range(J // STORE)]
+        o_words = [keep.tile([P, STORE], I32, name=f"o_words{s}", align_bytes=64) for s in range(J // STORE)]
+        o_scales = keep.tile([P, J], U8, name="o_scales", align_bytes=64)
+
+        ub, th, y, hb, ob = {}, {}, {}, {}, {}
+
+        def last_plane(c):
+            gather(g23[c][:, 1, :], 3, c * W, (c + 1) * W)
+            weave(nc.scalar.copy, xb[c][:, :, 2:4], g23[c][:])
+
+        def first_products(c):
+            words = ring.tile([P, W], I32, name="x_words", align_bytes=64)
+            scales = ring.tile([P, W], U8, name="x_scales", align_bytes=64)
+            quantize(words[:], scales[:], xb[c][:])
+            ga = psum.tile([P, PACK, W], F32, name="ga", bufs=3)
+            ub[c] = psum.tile([P, PACK, W], F32, name="ub", bufs=3)
+            product(ga, w1_words[0], w1_scales[:, :], words[:], scales[:])
+            product(ub[c], w1_words[1], w1_scales[4:, :], words[:], scales[:])
+            th[c] = ring.tile([P, W, PACK], F32, name="th")
+            nc.scalar.activation(th[c][:], ga[:].rearrange("p t j -> p j t"), TANH)
+
+        def gate(c):
+            hb[c] = ring.tile([P, W, PACK], BF16, name="hb", align_bytes=64, bufs=CHUNKS)
+            nc.vector.tensor_tensor(hb[c][:], ub[c][:].rearrange("p t j -> p j t"), th[c][:], MULT)
+
+        def second_product(c):
+            words = ring.tile([P, W], I32, name="h_words", align_bytes=64, bufs=CHUNKS)
+            scales = ring.tile([P, W], U8, name="h_scales", align_bytes=64, bufs=CHUNKS)
+            quantize(words[:], scales[:], hb[c][:])
+            y[c] = psum.tile([P, PACK, W], F32, name="y", bufs=2)
+            product(y[c], wd_words, wd_scales[:, :], words[:], scales[:])
+
+        def residual(c):
+            s, a = divmod(c * W, STORE)
+            nc.vector.tensor_tensor(o32[s][:, :, a:a + W], y[c][:], res_sb[s][:, :, a:a + W], ADD)
+            ob[c] = ring.tile([P, W, PACK], BF16, name="ob", align_bytes=64)
+            weave(nc.vector.tensor_copy if c == CHUNKS - 1 else nc.scalar.copy, ob[c][:], o32[s][:, :, a:a + W])
+            if a + W == STORE:
+                nc.sync.dma_start(out_rows[:, :, s * STORE:(s + 1) * STORE], o32[s][:])
+
+        def planes_out(c):
+            s, a = divmod(c * W, STORE)
+            quantize(o_words[s][:, a:a + W], o_scales[:, c * W:(c + 1) * W], ob[c][:])
+            if a + W == STORE:
+                nc.sync.dma_start(out_words[:, s * STORE:(s + 1) * STORE], o_words[s][:])
+
+        stages = ((last_plane, 0), (first_products, 2), (gate, 4), (second_product, 5), (residual, 7), (planes_out, 8))
+        for step in range(CHUNKS + 8):
+            if step == 2:
+                deal_w1(0)
+                deal_w1(1)
+            if step == 5:
+                for k in range(4):
+                    deal_wd(k)
+                quantize(wd_words[:], wd_scales[:], wd_bf[:])
+            for stage, lag in reversed(stages):
+                if 0 <= step - lag < CHUNKS:
+                    stage(step - lag)
+
+        for q in range(4):
+            queue = nc.scalar if q % 2 else nc.sync
+            queue.dma_start(out_2[0, 4 * q:4 * q + 4, :].bitcast(I32), o_scales[32 * q:32 * q + 4, :].bitcast(I32))

@@ -19,8 +19,13 @@ P = 128
 PACK = 4
 W = 128
 CHUNKS = J // W
-STORE = 256
 LEAD = 256
+X_GROUPS = ((0,), (1,), (2, 3), (4, 5), (6, 7))
+H_GROUPS = ((0, 1), (2, 3), (4, 5), (6,), (7,))
+O_GROUPS = ((0, 1), (2, 3), (4, 5), (6,), (7,))
+RES_COLS = 256
+WD_PARTS = 4
+WD_ON_VECTOR = 1
 
 
 def tile_list_tanh_resP_kernel(tc, xT, wgt, wg_words, wg_scales, wu_words, wu_scales, wd, res, offs, out_0, out_1, out_2):
@@ -40,72 +45,45 @@ def tile_list_tanh_resP_kernel(tc, xT, wgt, wg_words, wg_scales, wu_words, wu_sc
         nc.sync.dma_start(wgt_lead[:], wgt[:, :LEAD])
         nc.sync.dma_start(planes[0][:], x_rows[0])
         nc.sync.dma_start(wgt_rest[:], wgt[:, LEAD:])
-        for i in range(1, PACK):
-            nc.sync.dma_start(planes[i][:], x_rows[i])
+        scales_raw = keep.tile([P, R], U8, name="scales_raw")
+        nc.vector.memset(scales_raw[:].bitcast(I32), 0)
 
+        def load_scales(first, scales):
+            for q in range(4):
+                nc.sync.dma_start(scales_raw[32 * q + first:32 * q + first + 4, :].bitcast(I32),
+                                  scales[0, 4 * q:4 * q + 4, :].bitcast(I32))
+
+        nc.sync.dma_start(planes[1][:], x_rows[1])
+        load_scales(0, wg_scales)
+        nc.sync.dma_start(planes[2][:], x_rows[2])
         raw_words = []
         for name, words in (("wg_raw", wg_words), ("wu_raw", wu_words)):
             raw = keep.tile([P, R], I32, name=name)
             nc.sync.dma_start(raw[:], words[0].rearrange("p r i -> p (r i)").bitcast(I32))
             raw_words.append(raw)
+        load_scales(4, wu_scales)
+        nc.sync.dma_start(planes[3][:], x_rows[3])
         wd_raw = keep.tile([P, PACK, N], F32, name="wd_raw")
-        nc.sync.dma_start(wd_raw[:], wd.rearrange("(p i) n -> p i n", i=PACK))
+        wd_rows = wd.rearrange("(q i s) n -> i q s n", i=PACK, s=8)
+        for i in range(PACK):
+            nc.sync.dma_start(wd_raw[:, i, :], wd_rows[i])
         res_rows = res.rearrange("(p t) j -> p t j", t=PACK)
         res_sb = []
-        for s in range(J // STORE):
-            part = keep.tile([P, PACK, STORE], F32, name=f"res{s}")
-            nc.sync.dma_start(part[:], res_rows[:, :, s * STORE:(s + 1) * STORE])
+        for s in range(J // RES_COLS):
+            part = keep.tile([P, PACK, RES_COLS], F32, name=f"res{s}")
+            nc.sync.dma_start(part[:], res_rows[:, :, s * RES_COLS:(s + 1) * RES_COLS])
             res_sb.append(part)
-
-        scales_raw = keep.tile([P, R], U8, name="scales_raw")
-        nc.gpsimd.memset(scales_raw[:].bitcast(I32), 0)
-        for first, scales in ((0, wg_scales), (4, wu_scales)):
-            for q in range(4):
-                nc.gpsimd.dma_start(scales_raw[32 * q + first:32 * q + first + 4, :].bitcast(I32),
-                                    scales[0, 4 * q:4 * q + 4, :].bitcast(I32))
 
         warm = keep.tile([P, 1], F32, name="warm")
         nc.vector.memset(warm[:], 0.0)
         nc.scalar.activation(warm[:], warm[:], TANH)
 
-        def wgt_cols(a, b):
-            return wgt_lead[:, a:b] if b <= LEAD else wgt_rest[:, a - LEAD:b - LEAD]
-
         def gather(out, i, a, b):
-            nc.vector.tensor_tensor(out, planes[i][:].indirect(offsets[:, a // 16:b // 16]), wgt_cols(a, b), MULT)
-
-        g01 = keep.tile([P, 2, J], F32, name="g01")
-        for i in range(2):
-            gather(g01[:, i, :LEAD], i, 0, LEAD)
-            gather(g01[:, i, LEAD:], i, LEAD, J)
-        g23 = [keep.tile([P, 2, W], F32, name=f"g23_{c}") for c in range(CHUNKS)]
-        xb = [keep.tile([P, W, PACK], BF16, name=f"xb{c}", align_bytes=64) for c in range(CHUNKS)]
+            weights = wgt_lead[:, a:b] if b <= LEAD else wgt_rest[:, a - LEAD:b - LEAD]
+            nc.vector.tensor_tensor(out, planes[i][:].indirect(offsets[:, a // 16:b // 16]), weights, MULT)
 
         def weave(engine_copy, dst, src):
             engine_copy(dst.rearrange("p (c i) t -> p c t i", i=4), src.rearrange("p t (c i) -> p c t i", i=4))
-
-        for c in range(CHUNKS):
-            weave(nc.scalar.copy, xb[c][:, :, 0:2], g01[:, :, c * W:(c + 1) * W])
-        for c in range(CHUNKS):
-            gather(g23[c][:, 0, :], 2, c * W, (c + 1) * W)
-
-        w1_words = [keep.tile([P, R], I32, name=f"w1_words{k}", align_bytes=64) for k in range(2)]
-        w1_scales = keep.tile([P, R], U8, name="w1_scales", align_bytes=64)
-        nc.vector.tensor_copy(w1_scales[:].rearrange("p (t c i) -> p c t i", t=4, i=16),
-                              scales_raw[:].rearrange("p (c i t) -> p c t i", t=4, i=16))
-
-        def deal_w1(k):
-            nc.vector.tensor_copy(w1_words[k][:].rearrange("p (t c i) -> p c t i", t=4, i=4),
-                                  raw_words[k][:].rearrange("p (c i t) -> p c t i", t=4, i=4))
-
-        wd_bf = keep.tile([P, N, PACK], BF16, name="wd_bf", align_bytes=64)
-        wd_words = keep.tile([P, N], I32, name="wd_words", align_bytes=64)
-        wd_scales = keep.tile([P, N], U8, name="wd_scales", align_bytes=64)
-
-        def deal_wd(k):
-            ms = slice(32 * k, 32 * (k + 1))
-            nc.scalar.copy(wd_bf[:].rearrange("p (t m) i -> p m i t", t=4)[:, ms],
-                           wd_raw[:].rearrange("p i (m t) -> p m i t", t=4)[:, ms])
 
         def quantize(words, scales, src):
             nc.vector.quantize_mx(out=words.bitcast(FP8X4), scales=scales, in_=src.rearrange("p j t -> p (j t)"))
@@ -116,62 +94,113 @@ def tile_list_tanh_resP_kernel(tc, xT, wgt, wg_words, wg_scales, wu_words, wu_sc
                 nc.tensor.matmul_mx(out=bank[:, t, :], lhsT=words[:, cols].bitcast(FP8X4), lhsT_scale=scales[:, cols],
                                     rhs=rhs.bitcast(FP8X4), rhs_scale=rhs_scale, start=True, stop=True)
 
+        def place(groups, c):
+            g = next_group = 0
+            for g, chunks in enumerate(groups):
+                if c in chunks:
+                    next_group = chunks.index(c)
+                    break
+            return g, slice(next_group * W, (next_group + 1) * W)
+
+        g01 = keep.tile([P, 2, J], F32, name="g01")
+        for i in range(2):
+            gather(g01[:, i, :LEAD], i, 0, LEAD)
+            gather(g01[:, i, LEAD:], i, LEAD, J)
+        g23 = [keep.tile([P, 2, W * len(g)], F32, name=f"g23_{k}") for k, g in enumerate(X_GROUPS)]
+        xb = [keep.tile([P, W * len(g), PACK], BF16, name=f"xb{k}", align_bytes=64) for k, g in enumerate(X_GROUPS)]
+        for k, g in enumerate(X_GROUPS):
+            weave(nc.scalar.copy, xb[k][:, :, 0:2], g01[:, :, g[0] * W:(g[-1] + 1) * W])
+        for k, g in enumerate(X_GROUPS):
+            gather(g23[k][:, 0, :], 2, g[0] * W, (g[-1] + 1) * W)
+
+        w1_words = [keep.tile([P, R], I32, name=f"w1_words{k}", align_bytes=64) for k in range(2)]
+        w1_scales = keep.tile([P, R], U8, name="w1_scales", align_bytes=64)
+        for k in range(2):
+            nc.vector.tensor_copy(w1_words[k][:].rearrange("p (t q s) -> p q t s", t=4, s=8),
+                                  raw_words[k][:].rearrange("p (q t s) -> p q t s", t=4, s=8))
+        nc.vector.tensor_copy(w1_scales[:].bitcast(I32).rearrange("p (t q s) -> p t q s", t=4, s=2),
+                              scales_raw[:].bitcast(I32).rearrange("p (q t s) -> p t q s", t=4, s=2))
+
+        wd_bf = keep.tile([P, N, PACK], BF16, name="wd_bf", align_bytes=64)
+        wd_words = keep.tile([P, N], I32, name="wd_words", align_bytes=64)
+        wd_scales = keep.tile([P, N], U8, name="wd_scales", align_bytes=64)
+
+        def deal_wd(k):
+            ms = slice(P // WD_PARTS * k, P // WD_PARTS * (k + 1))
+            copy = nc.vector.tensor_copy if k >= WD_PARTS - WD_ON_VECTOR else nc.scalar.copy
+            copy(wd_bf[:].rearrange("p (t m) i -> p m i t", t=4)[:, ms],
+                 wd_raw[:].rearrange("p i (m t) -> p m i t", t=4)[:, ms])
+
         out_rows = out_0.rearrange("(p t) j -> p t j", t=PACK)
         out_words = out_1[0].rearrange("p j i -> p (j i)").bitcast(I32)
-        o32 = [keep.tile([P, PACK, STORE], F32, name=f"o32_{s}") for s in range(J // STORE)]
-        o_words = [keep.tile([P, STORE], I32, name=f"o_words{s}", align_bytes=64) for s in range(J // STORE)]
         o_scales = keep.tile([P, J], U8, name="o_scales", align_bytes=64)
 
-        ub, th, y, hb, ob = {}, {}, {}, {}, {}
+        def group_tiles(groups, name, shape_of, dtype):
+            return [keep.tile(shape_of(W * len(g)), dtype, name=f"{name}{k}", align_bytes=64) for k, g in enumerate(groups)]
+
+        x_words = group_tiles(X_GROUPS, "x_words", lambda w: [P, w], I32)
+        x_scales = group_tiles(X_GROUPS, "x_scales", lambda w: [P, w], U8)
+        hb = group_tiles(H_GROUPS, "hb", lambda w: [P, w, PACK], BF16)
+        h_words = group_tiles(H_GROUPS, "h_words", lambda w: [P, w], I32)
+        h_scales = group_tiles(H_GROUPS, "h_scales", lambda w: [P, w], U8)
+        o32 = group_tiles(O_GROUPS, "o32", lambda w: [P, PACK, w], F32)
+        ob = group_tiles(O_GROUPS, "ob", lambda w: [P, w, PACK], BF16)
+        o_words = group_tiles(O_GROUPS, "o_words", lambda w: [P, w], I32)
+        ub, th, y = {}, {}, {}
 
         def last_plane(c):
-            gather(g23[c][:, 1, :], 3, c * W, (c + 1) * W)
-            weave(nc.scalar.copy, xb[c][:, :, 2:4], g23[c][:])
+            k, cols = place(X_GROUPS, c)
+            g = X_GROUPS[k]
+            if c == g[0]:
+                gather(g23[k][:, 1, :], 3, g[0] * W, (g[-1] + 1) * W)
+                weave(nc.scalar.copy, xb[k][:, :, 2:4], g23[k][:])
 
         def first_products(c):
-            words = ring.tile([P, W], I32, name="x_words", align_bytes=64)
-            scales = ring.tile([P, W], U8, name="x_scales", align_bytes=64)
-            quantize(words[:], scales[:], xb[c][:])
-            ga = psum.tile([P, PACK, W], F32, name="ga", bufs=3)
+            k, cols = place(X_GROUPS, c)
+            if c == X_GROUPS[k][0]:
+                quantize(x_words[k][:], x_scales[k][:], xb[k][:])
+            ga = psum.tile([P, PACK, W], F32, name="ga", bufs=2)
             ub[c] = psum.tile([P, PACK, W], F32, name="ub", bufs=3)
-            product(ga, w1_words[0], w1_scales[:, :], words[:], scales[:])
-            product(ub[c], w1_words[1], w1_scales[4:, :], words[:], scales[:])
+            product(ga, w1_words[0], w1_scales[:, :], x_words[k][:, cols], x_scales[k][:, cols])
+            product(ub[c], w1_words[1], w1_scales[4:, :], x_words[k][:, cols], x_scales[k][:, cols])
             th[c] = ring.tile([P, W, PACK], F32, name="th")
             nc.scalar.activation(th[c][:], ga[:].rearrange("p t j -> p j t"), TANH)
 
         def gate(c):
-            hb[c] = ring.tile([P, W, PACK], BF16, name="hb", align_bytes=64, bufs=CHUNKS)
-            nc.vector.tensor_tensor(hb[c][:], ub[c][:].rearrange("p t j -> p j t"), th[c][:], MULT)
+            k, cols = place(H_GROUPS, c)
+            nc.vector.tensor_tensor(hb[k][:, cols, :], ub[c][:].rearrange("p t j -> p j t"), th[c][:], MULT)
+
+        def quantize_h(c):
+            k, cols = place(H_GROUPS, c)
+            if c == H_GROUPS[k][-1]:
+                quantize(h_words[k][:], h_scales[k][:], hb[k][:])
 
         def second_product(c):
-            words = ring.tile([P, W], I32, name="h_words", align_bytes=64, bufs=CHUNKS)
-            scales = ring.tile([P, W], U8, name="h_scales", align_bytes=64, bufs=CHUNKS)
-            quantize(words[:], scales[:], hb[c][:])
-            y[c] = psum.tile([P, PACK, W], F32, name="y", bufs=2)
-            product(y[c], wd_words, wd_scales[:, :], words[:], scales[:])
+            k, cols = place(H_GROUPS, c)
+            y[c] = psum.tile([P, PACK, W], F32, name="y", bufs=3)
+            product(y[c], wd_words, wd_scales[:, :], h_words[k][:, cols], h_scales[k][:, cols])
 
         def residual(c):
-            s, a = divmod(c * W, STORE)
-            nc.vector.tensor_tensor(o32[s][:, :, a:a + W], y[c][:], res_sb[s][:, :, a:a + W], ADD)
-            ob[c] = ring.tile([P, W, PACK], BF16, name="ob", align_bytes=64)
-            weave(nc.vector.tensor_copy if c == CHUNKS - 1 else nc.scalar.copy, ob[c][:], o32[s][:, :, a:a + W])
-            if a + W == STORE:
-                nc.sync.dma_start(out_rows[:, :, s * STORE:(s + 1) * STORE], o32[s][:])
+            k, cols = place(O_GROUPS, c)
+            g = O_GROUPS[k]
+            s, a = divmod(c * W, RES_COLS)
+            nc.vector.tensor_tensor(o32[k][:, :, cols], y[c][:], res_sb[s][:, :, a:a + W], ADD)
+            weave(nc.vector.tensor_copy if c == CHUNKS - 1 else nc.scalar.copy, ob[k][:, cols, :], o32[k][:, :, cols])
+            if c == g[-1]:
+                nc.sync.dma_start(out_rows[:, :, g[0] * W:(c + 1) * W], o32[k][:])
 
         def planes_out(c):
-            s, a = divmod(c * W, STORE)
-            quantize(o_words[s][:, a:a + W], o_scales[:, c * W:(c + 1) * W], ob[c][:])
-            if a + W == STORE:
-                nc.sync.dma_start(out_words[:, s * STORE:(s + 1) * STORE], o_words[s][:])
+            k, cols = place(O_GROUPS, c)
+            g = O_GROUPS[k]
+            if c == g[-1]:
+                quantize(o_words[k][:], o_scales[:, g[0] * W:(c + 1) * W], ob[k][:])
+                nc.sync.dma_start(out_words[:, g[0] * W:(c + 1) * W], o_words[k][:])
 
-        stages = ((last_plane, 0), (first_products, 2), (gate, 4), (second_product, 5), (residual, 7), (planes_out, 8))
-        for step in range(CHUNKS + 8):
-            if step == 2:
-                deal_w1(0)
-                deal_w1(1)
-            if step == 5:
-                for k in range(4):
-                    deal_wd(k)
+        stages = ((last_plane, 0), (first_products, 2), (gate, 4), (quantize_h, 5), (second_product, 8), (residual, 9), (planes_out, 10))
+        for step in range(CHUNKS + 10):
+            if 0 <= step - 4 < WD_PARTS:
+                deal_wd(step - 4)
+            if step == 8:
                 quantize(wd_words[:], wd_scales[:], wd_bf[:])
             for stage, lag in reversed(stages):
                 if 0 <= step - lag < CHUNKS:

@@ -19,13 +19,15 @@ P = 128
 PACK = 4
 W = 128
 CHUNKS = J // W
-LEAD = 256
-X_GROUPS = ((0,), (1,), (2, 3), (4, 5), (6, 7))
-H_GROUPS = ((0, 1), (2, 3), (4, 5), (6,), (7,))
-O_GROUPS = ((0, 1), (2, 3), (4, 5), (6,), (7,))
+LEAD = 512
+S_GROUPS = ((0, 1), (2, 3), (4, 5), (6, 7))
+WORD_STORES = ((0, 1, 2, 3), (4, 5, 6, 7))
+X_GROUPS = ((0,), (1,), (2,), (3,), (4, 5), (6, 7))
+H_GROUPS = tuple((c,) for c in range(CHUNKS))
+O_GROUPS = ((0, 1), (2, 3), (4, 5), (6, 7))
 RES_COLS = 256
 WD_PARTS = 4
-WD_ON_VECTOR = 1
+WD_ON_VECTOR = 2
 
 
 def tile_list_tanh_resP_kernel(tc, xT, wgt, wg_words, wg_scales, wu_words, wu_scales, wd, res, offs, out_0, out_1, out_2):
@@ -35,16 +37,14 @@ def tile_list_tanh_resP_kernel(tc, xT, wgt, wg_words, wg_scales, wu_words, wu_sc
         ring = ctx.enter_context(tc.tile_pool(name="ring", bufs=3))
         psum = ctx.enter_context(tc.psum_pool(name="psum", bufs=1))
 
+        wgt_cut = keep.tile([P, W], F32, name="wgt_cut", align_bytes=64)
+        nc.sync.dma_start(wgt_cut[:], wgt.rearrange("(a r) (s c) -> r a s c", r=8, c=W)[0])
         offsets = keep.tile([P, J // 16], U16, name="offsets")
-        nc.sync.dma_start(offsets[:], offs)
 
         x_rows = xT.rearrange("(p i) t -> i p t", i=PACK)
         planes = [keep.tile([P, T], F32, name=f"plane{i}") for i in range(PACK)]
-        wgt_lead = keep.tile([P, LEAD], F32, name="wgt_lead")
-        wgt_rest = keep.tile([P, J - LEAD], F32, name="wgt_rest")
-        nc.sync.dma_start(wgt_lead[:], wgt[:, :LEAD])
         nc.sync.dma_start(planes[0][:], x_rows[0])
-        nc.sync.dma_start(wgt_rest[:], wgt[:, LEAD:])
+        nc.sync.dma_start(offsets[:], offs)
         scales_raw = keep.tile([P, R], U8, name="scales_raw")
         nc.vector.memset(scales_raw[:].bitcast(I32), 0)
 
@@ -78,6 +78,19 @@ def tile_list_tanh_resP_kernel(tc, xT, wgt, wg_words, wg_scales, wu_words, wu_sc
         nc.vector.memset(warm[:], 0.0)
         nc.scalar.activation(warm[:], warm[:], TANH)
 
+        wgt_turned = keep.tile([P, W], F32, name="wgt_turned", align_bytes=64)
+        nc.vector.transpose(wgt_turned[:], wgt_cut[:])
+        by_head = wgt_turned[:].rearrange("p (b h d s) -> p s b h d", b=4, h=2, d=2)
+        halves = []
+        for half, copy in enumerate((nc.vector.tensor_copy, nc.scalar.copy)):
+            spread = keep.tile([P, LEAD], F32, name=f"wgt_spread{half}", align_bytes=64)
+            copy(spread[:].rearrange("p (s b h r) -> p s b h r", s=4, b=4, h=2),
+                 by_head[:, 4 * half:4 * half + 4, :, :, 0:1].to_broadcast([P, 4, 4, 2, 16]))
+            full = keep.tile([P, LEAD], F32, name=f"wgt_full{half}", align_bytes=64)
+            nc.vector.transpose(full[:], spread[:])
+            halves.append(full)
+        wgt_lead, wgt_rest = halves
+
         def gather(out, i, a, b):
             weights = wgt_lead[:, a:b] if b <= LEAD else wgt_rest[:, a - LEAD:b - LEAD]
             nc.vector.tensor_tensor(out, planes[i][:].indirect(offsets[:, a // 16:b // 16]), weights, MULT)
@@ -109,7 +122,7 @@ def tile_list_tanh_resP_kernel(tc, xT, wgt, wg_words, wg_scales, wu_words, wu_sc
         g23 = [keep.tile([P, 2, W * len(g)], F32, name=f"g23_{k}") for k, g in enumerate(X_GROUPS)]
         xb = [keep.tile([P, W * len(g), PACK], BF16, name=f"xb{k}", align_bytes=64) for k, g in enumerate(X_GROUPS)]
         for k, g in enumerate(X_GROUPS):
-            weave(nc.scalar.copy, xb[k][:, :, 0:2], g01[:, :, g[0] * W:(g[-1] + 1) * W])
+            nc.scalar.copy(xb[k][:, :, 0:2], g01[:, :, g[0] * W:(g[-1] + 1) * W].rearrange("p t j -> p j t"))
         for k, g in enumerate(X_GROUPS):
             gather(g23[k][:, 0, :], 2, g[0] * W, (g[-1] + 1) * W)
 
@@ -143,9 +156,9 @@ def tile_list_tanh_resP_kernel(tc, xT, wgt, wg_words, wg_scales, wu_words, wu_sc
         hb = group_tiles(H_GROUPS, "hb", lambda w: [P, w, PACK], BF16)
         h_words = group_tiles(H_GROUPS, "h_words", lambda w: [P, w], I32)
         h_scales = group_tiles(H_GROUPS, "h_scales", lambda w: [P, w], U8)
-        o32 = group_tiles(O_GROUPS, "o32", lambda w: [P, PACK, w], F32)
+        o32 = group_tiles(S_GROUPS, "o32", lambda w: [P, PACK, w], F32)
         ob = group_tiles(O_GROUPS, "ob", lambda w: [P, w, PACK], BF16)
-        o_words = group_tiles(O_GROUPS, "o_words", lambda w: [P, w], I32)
+        o_words = group_tiles(WORD_STORES, "o_words", lambda w: [P, w], I32)
         ub, th, y = {}, {}, {}
 
         def last_plane(c):
@@ -153,13 +166,13 @@ def tile_list_tanh_resP_kernel(tc, xT, wgt, wg_words, wg_scales, wu_words, wu_sc
             g = X_GROUPS[k]
             if c == g[0]:
                 gather(g23[k][:, 1, :], 3, g[0] * W, (g[-1] + 1) * W)
-                weave(nc.scalar.copy, xb[k][:, :, 2:4], g23[k][:])
+                nc.scalar.copy(xb[k][:, :, 2:4], g23[k][:].rearrange("p t j -> p j t"))
 
         def first_products(c):
             k, cols = place(X_GROUPS, c)
             if c == X_GROUPS[k][0]:
                 quantize(x_words[k][:], x_scales[k][:], xb[k][:])
-            ga = psum.tile([P, PACK, W], F32, name="ga", bufs=2)
+            ga = psum.tile([P, PACK, W], F32, name="ga", bufs=3)
             ub[c] = psum.tile([P, PACK, W], F32, name="ub", bufs=3)
             product(ga, w1_words[0], w1_scales[:, :], x_words[k][:, cols], x_scales[k][:, cols])
             product(ub[c], w1_words[1], w1_scales[4:, :], x_words[k][:, cols], x_scales[k][:, cols])
@@ -177,15 +190,16 @@ def tile_list_tanh_resP_kernel(tc, xT, wgt, wg_words, wg_scales, wu_words, wu_sc
 
         def second_product(c):
             k, cols = place(H_GROUPS, c)
-            y[c] = psum.tile([P, PACK, W], F32, name="y", bufs=3)
+            y[c] = psum.tile([P, PACK, W], F32, name="y", bufs=2)
             product(y[c], wd_words, wd_scales[:, :], h_words[k][:, cols], h_scales[k][:, cols])
 
         def residual(c):
-            k, cols = place(O_GROUPS, c)
-            g = O_GROUPS[k]
+            k, cols = place(S_GROUPS, c)
+            g = S_GROUPS[k]
+            ko, ocols = place(O_GROUPS, c)
             s, a = divmod(c * W, RES_COLS)
             nc.vector.tensor_tensor(o32[k][:, :, cols], y[c][:], res_sb[s][:, :, a:a + W], ADD)
-            weave(nc.vector.tensor_copy if c == CHUNKS - 1 else nc.scalar.copy, ob[k][:, cols, :], o32[k][:, :, cols])
+            weave(nc.vector.tensor_copy if c == CHUNKS - 1 else nc.scalar.copy, ob[ko][:, ocols, :], o32[k][:, :, cols])
             if c == g[-1]:
                 nc.sync.dma_start(out_rows[:, :, g[0] * W:(c + 1) * W], o32[k][:])
 
@@ -193,14 +207,17 @@ def tile_list_tanh_resP_kernel(tc, xT, wgt, wg_words, wg_scales, wu_words, wu_sc
             k, cols = place(O_GROUPS, c)
             g = O_GROUPS[k]
             if c == g[-1]:
-                quantize(o_words[k][:], o_scales[:, g[0] * W:(c + 1) * W], ob[k][:])
-                nc.sync.dma_start(out_words[:, g[0] * W:(c + 1) * W], o_words[k][:])
+                kw, last = place(WORD_STORES, c)
+                quantize(o_words[kw][:, last.stop - len(g) * W:last.stop], o_scales[:, g[0] * W:(c + 1) * W], ob[k][:])
+                if c == WORD_STORES[kw][-1]:
+                    nc.sync.dma_start(out_words[:, WORD_STORES[kw][0] * W:(c + 1) * W], o_words[kw][:])
 
-        stages = ((last_plane, 0), (first_products, 2), (gate, 4), (quantize_h, 5), (second_product, 8), (residual, 9), (planes_out, 10))
-        for step in range(CHUNKS + 10):
-            if 0 <= step - 4 < WD_PARTS:
-                deal_wd(step - 4)
-            if step == 8:
+        stages = ((last_plane, 0), (first_products, 1), (gate, 2), (quantize_h, 3), (second_product, 4), (residual, 5), (planes_out, 7))
+        for step in range(CHUNKS + 7):
+            if step == 0:
+                for k in range(WD_PARTS):
+                    deal_wd(k)
+            if step == 1:
                 quantize(wd_words[:], wd_scales[:], wd_bf[:])
             for stage, lag in reversed(stages):
                 if 0 <= step - lag < CHUNKS:

@@ -19,31 +19,38 @@ P = 128
 PACK = 4
 W = 128
 CHUNKS = J // W
-LEAD = 512
+X_GROUPS = ((0,), (1,), (2, 3), (4, 5), (6, 7))
+H_GROUPS = ((0, 1), (2, 3), (4, 5), (6, 7))
+E_GROUPS = tuple((c,) for c in range(CHUNKS))
+F_GROUPS = tuple((c,) for c in range(CHUNKS))
+O_GROUPS = ((0, 1, 2, 3), (4, 5), (6,), (7,))
 S_GROUPS = ((0, 1), (2, 3), (4, 5), (6, 7))
 WORD_STORES = ((0, 1, 2, 3), (4, 5, 6, 7))
-X_GROUPS = ((0,), (1,), (2,), (3,), (4, 5), (6, 7))
-H_GROUPS = tuple((c,) for c in range(CHUNKS))
-O_GROUPS = ((0, 1), (2, 3), (4, 5), (6, 7))
-RES_COLS = 256
-WD_PARTS = 4
-WD_ON_VECTOR = 2
+RES_COLS = 1024
+
+
+def span(chunks):
+    return slice(chunks[0] * W, (chunks[-1] + 1) * W)
+
+
+def place(groups, chunks):
+    k = [g for g, members in enumerate(groups) if chunks[0] in members][0]
+    first = groups[k][0] * W
+    return k, slice(chunks[0] * W - first, (chunks[-1] + 1) * W - first)
 
 
 def tile_list_tanh_resP_kernel(tc, xT, wgt, wg_words, wg_scales, wu_words, wu_scales, wd, res, offs, out_0, out_1, out_2):
     nc = tc.nc
     with ExitStack() as ctx:
         keep = ctx.enter_context(tc.tile_pool(name="keep", bufs=1))
-        ring = ctx.enter_context(tc.tile_pool(name="ring", bufs=3))
         psum = ctx.enter_context(tc.psum_pool(name="psum", bufs=1))
 
         wgt_cut = keep.tile([P, W], F32, name="wgt_cut", align_bytes=64)
         nc.sync.dma_start(wgt_cut[:], wgt.rearrange("(a r) (s c) -> r a s c", r=8, c=W)[0])
-        offsets = keep.tile([P, J // 16], U16, name="offsets")
-
         x_rows = xT.rearrange("(p i) t -> i p t", i=PACK)
         planes = [keep.tile([P, T], F32, name=f"plane{i}") for i in range(PACK)]
         nc.sync.dma_start(planes[0][:], x_rows[0])
+        offsets = keep.tile([P, J // 16], U16, name="offsets")
         nc.sync.dma_start(offsets[:], offs)
         scales_raw = keep.tile([P, R], U8, name="scales_raw")
         nc.vector.memset(scales_raw[:].bitcast(I32), 0)
@@ -56,11 +63,9 @@ def tile_list_tanh_resP_kernel(tc, xT, wgt, wg_words, wg_scales, wu_words, wu_sc
         nc.sync.dma_start(planes[1][:], x_rows[1])
         load_scales(0, wg_scales)
         nc.sync.dma_start(planes[2][:], x_rows[2])
-        raw_words = []
-        for name, words in (("wg_raw", wg_words), ("wu_raw", wu_words)):
-            raw = keep.tile([P, R], I32, name=name)
-            nc.sync.dma_start(raw[:], words[0].rearrange("p r i -> p (r i)").bitcast(I32))
-            raw_words.append(raw)
+        words_raw = keep.tile([P, 2, R], I32, name="words_raw")
+        for k, words in enumerate((wg_words, wu_words)):
+            nc.sync.dma_start(words_raw[:, k, :], words[0].rearrange("p r i -> p (r i)").bitcast(I32))
         load_scales(4, wu_scales)
         nc.sync.dma_start(planes[3][:], x_rows[3])
         wd_raw = keep.tile([P, PACK, N], F32, name="wd_raw")
@@ -81,56 +86,49 @@ def tile_list_tanh_resP_kernel(tc, xT, wgt, wg_words, wg_scales, wu_words, wu_sc
         wgt_turned = keep.tile([P, W], F32, name="wgt_turned", align_bytes=64)
         nc.vector.transpose(wgt_turned[:], wgt_cut[:])
         by_head = wgt_turned[:].rearrange("p (b h d s) -> p s b h d", b=4, h=2, d=2)
-        halves = []
-        for half, copy in enumerate((nc.vector.tensor_copy, nc.scalar.copy)):
-            spread = keep.tile([P, LEAD], F32, name=f"wgt_spread{half}", align_bytes=64)
-            copy(spread[:].rearrange("p (s b h r) -> p s b h r", s=4, b=4, h=2),
-                 by_head[:, 4 * half:4 * half + 4, :, :, 0:1].to_broadcast([P, 4, 4, 2, 16]))
-            full = keep.tile([P, LEAD], F32, name=f"wgt_full{half}", align_bytes=64)
-            nc.vector.transpose(full[:], spread[:])
-            halves.append(full)
-        wgt_lead, wgt_rest = halves
+        wgt_full = keep.tile([P, J], F32, name="wgt_full", align_bytes=64)
+        pieces = ((0, 2, nc.vector.tensor_copy), (2, 4, nc.vector.tensor_copy), (4, 8, nc.scalar.copy))
+        spread = [keep.tile([P, (b - a) * W], F32, name=f"wgt_spread{a}", align_bytes=64) for a, b, copy in pieces]
+        for tile, (a, b, copy) in zip(spread, pieces):
+            copy(tile[:].rearrange("p (s b h r) -> p s b h r", b=4, h=2, r=16),
+                 by_head[:, a:b, :, :, 0:1].to_broadcast([P, b - a, 4, 2, 16]))
+        for tile, (a, b, copy) in zip(spread, pieces):
+            nc.vector.transpose(wgt_full[:, a * W:b * W], tile[:])
 
-        def gather(out, i, a, b):
-            weights = wgt_lead[:, a:b] if b <= LEAD else wgt_rest[:, a - LEAD:b - LEAD]
-            nc.vector.tensor_tensor(out, planes[i][:].indirect(offsets[:, a // 16:b // 16]), weights, MULT)
+        def gather(out, i, cols):
+            nc.vector.tensor_tensor(out, planes[i][:].indirect(offsets[:, cols.start // 16:cols.stop // 16]),
+                                    wgt_full[:, cols], MULT)
 
         def weave(engine_copy, dst, src):
-            engine_copy(dst.rearrange("p (c i) t -> p c t i", i=4), src.rearrange("p t (c i) -> p c t i", i=4))
+            engine_copy(dst.rearrange("p (c i) t -> p c t i", i=2), src.rearrange("p t (c i) -> p c t i", i=2))
 
         def quantize(words, scales, src):
             nc.vector.quantize_mx(out=words.bitcast(FP8X4), scales=scales, in_=src.rearrange("p j t -> p (j t)"))
 
-        def product(bank, words, scales, rhs, rhs_scale):
+        def product(out, words, scales, rhs, rhs_scale):
             for t in range(PACK):
                 cols = slice(t * P, (t + 1) * P)
-                nc.tensor.matmul_mx(out=bank[:, t, :], lhsT=words[:, cols].bitcast(FP8X4), lhsT_scale=scales[:, cols],
+                nc.tensor.matmul_mx(out=out[:, t, :], lhsT=words[:, cols].bitcast(FP8X4), lhsT_scale=scales[:, cols],
                                     rhs=rhs.bitcast(FP8X4), rhs_scale=rhs_scale, start=True, stop=True)
 
-        def place(groups, c):
-            g = next_group = 0
-            for g, chunks in enumerate(groups):
-                if c in chunks:
-                    next_group = chunks.index(c)
-                    break
-            return g, slice(next_group * W, (next_group + 1) * W)
+        def group_tiles(groups, name, shape_of, dtype):
+            return [keep.tile(shape_of(W * len(g)), dtype, name=f"{name}{k}", align_bytes=64) for k, g in enumerate(groups)]
 
         g01 = keep.tile([P, 2, J], F32, name="g01")
-        for i in range(2):
-            gather(g01[:, i, :LEAD], i, 0, LEAD)
-            gather(g01[:, i, LEAD:], i, LEAD, J)
-        g23 = [keep.tile([P, 2, W * len(g)], F32, name=f"g23_{k}") for k, g in enumerate(X_GROUPS)]
-        xb = [keep.tile([P, W * len(g), PACK], BF16, name=f"xb{k}", align_bytes=64) for k, g in enumerate(X_GROUPS)]
+        gather(g01[:, 0, :J // 2], 0, slice(0, J // 2))
+        gather(g01[:, 0, J // 2:], 0, slice(J // 2, J))
+        gather(g01[:, 1, :], 1, slice(0, J))
+        g23 = group_tiles(X_GROUPS, "g23_", lambda w: [P, 2, w], F32)
+        xb = group_tiles(X_GROUPS, "xb", lambda w: [P, w, PACK], BF16)
         for k, g in enumerate(X_GROUPS):
-            nc.scalar.copy(xb[k][:, :, 0:2], g01[:, :, g[0] * W:(g[-1] + 1) * W].rearrange("p t j -> p j t"))
+            nc.scalar.copy(xb[k][:, :, 0:2], g01[:, :, span(g)].rearrange("p t j -> p j t"))
         for k, g in enumerate(X_GROUPS):
-            gather(g23[k][:, 0, :], 2, g[0] * W, (g[-1] + 1) * W)
+            gather(g23[k][:, 0, :], 2, span(g))
 
-        w1_words = [keep.tile([P, R], I32, name=f"w1_words{k}", align_bytes=64) for k in range(2)]
+        w1_words = keep.tile([P, 2, R], I32, name="w1_words", align_bytes=64)
         w1_scales = keep.tile([P, R], U8, name="w1_scales", align_bytes=64)
-        for k in range(2):
-            nc.vector.tensor_copy(w1_words[k][:].rearrange("p (t q s) -> p q t s", t=4, s=8),
-                                  raw_words[k][:].rearrange("p (q t s) -> p q t s", t=4, s=8))
+        nc.vector.tensor_copy(w1_words[:].rearrange("p k (t q s) -> p k q t s", t=4, s=8),
+                              words_raw[:].rearrange("p k (q t s) -> p k q t s", t=4, s=8))
         nc.vector.tensor_copy(w1_scales[:].bitcast(I32).rearrange("p (t q s) -> p t q s", t=4, s=2),
                               scales_raw[:].bitcast(I32).rearrange("p (q t s) -> p t q s", t=4, s=2))
 
@@ -138,19 +136,9 @@ def tile_list_tanh_resP_kernel(tc, xT, wgt, wg_words, wg_scales, wu_words, wu_sc
         wd_words = keep.tile([P, N], I32, name="wd_words", align_bytes=64)
         wd_scales = keep.tile([P, N], U8, name="wd_scales", align_bytes=64)
 
-        def deal_wd(k):
-            ms = slice(P // WD_PARTS * k, P // WD_PARTS * (k + 1))
-            copy = nc.vector.tensor_copy if k >= WD_PARTS - WD_ON_VECTOR else nc.scalar.copy
-            copy(wd_bf[:].rearrange("p (t m) i -> p m i t", t=4)[:, ms],
-                 wd_raw[:].rearrange("p i (m t) -> p m i t", t=4)[:, ms])
-
         out_rows = out_0.rearrange("(p t) j -> p t j", t=PACK)
         out_words = out_1[0].rearrange("p j i -> p (j i)").bitcast(I32)
         o_scales = keep.tile([P, J], U8, name="o_scales", align_bytes=64)
-
-        def group_tiles(groups, name, shape_of, dtype):
-            return [keep.tile(shape_of(W * len(g)), dtype, name=f"{name}{k}", align_bytes=64) for k, g in enumerate(groups)]
-
         x_words = group_tiles(X_GROUPS, "x_words", lambda w: [P, w], I32)
         x_scales = group_tiles(X_GROUPS, "x_scales", lambda w: [P, w], U8)
         hb = group_tiles(H_GROUPS, "hb", lambda w: [P, w, PACK], BF16)
@@ -162,61 +150,69 @@ def tile_list_tanh_resP_kernel(tc, xT, wgt, wg_words, wg_scales, wu_words, wu_sc
         ub, th, y = {}, {}, {}
 
         def last_plane(c):
-            k, cols = place(X_GROUPS, c)
-            g = X_GROUPS[k]
-            if c == g[0]:
-                gather(g23[k][:, 1, :], 3, g[0] * W, (g[-1] + 1) * W)
+            k, cols = place(X_GROUPS, (c,))
+            if cols.start == 0:
+                gather(g23[k][:, 1, :], 3, span(X_GROUPS[k]))
                 nc.scalar.copy(xb[k][:, :, 2:4], g23[k][:].rearrange("p t j -> p j t"))
 
         def first_products(c):
-            k, cols = place(X_GROUPS, c)
-            if c == X_GROUPS[k][0]:
+            k, cols = place(X_GROUPS, (c,))
+            if cols.start == 0:
                 quantize(x_words[k][:], x_scales[k][:], xb[k][:])
-            ga = psum.tile([P, PACK, W], F32, name="ga", bufs=3)
+            ga = psum.tile([P, PACK, W], F32, name="ga", bufs=2)
             ub[c] = psum.tile([P, PACK, W], F32, name="ub", bufs=3)
-            product(ga, w1_words[0], w1_scales[:, :], x_words[k][:, cols], x_scales[k][:, cols])
-            product(ub[c], w1_words[1], w1_scales[4:, :], x_words[k][:, cols], x_scales[k][:, cols])
-            th[c] = ring.tile([P, W, PACK], F32, name="th")
+            product(ub[c], w1_words[:, 1, :], w1_scales[4:, :], x_words[k][:, cols], x_scales[k][:, cols])
+            product(ga, w1_words[:, 0, :], w1_scales[:, :], x_words[k][:, cols], x_scales[k][:, cols])
+            th[c] = keep.tile([P, W, PACK], F32, name=f"th{c}")
             nc.scalar.activation(th[c][:], ga[:].rearrange("p t j -> p j t"), TANH)
 
         def gate(c):
-            k, cols = place(H_GROUPS, c)
+            k, cols = place(H_GROUPS, (c,))
             nc.vector.tensor_tensor(hb[k][:, cols, :], ub[c][:].rearrange("p t j -> p j t"), th[c][:], MULT)
 
         def quantize_h(c):
-            k, cols = place(H_GROUPS, c)
+            k, cols = place(H_GROUPS, (c,))
             if c == H_GROUPS[k][-1]:
                 quantize(h_words[k][:], h_scales[k][:], hb[k][:])
 
         def second_product(c):
-            k, cols = place(H_GROUPS, c)
-            y[c] = psum.tile([P, PACK, W], F32, name="y", bufs=2)
-            product(y[c], wd_words, wd_scales[:, :], h_words[k][:, cols], h_scales[k][:, cols])
+            k, cols = place(H_GROUPS, (c,))
+            e, ecols = place(E_GROUPS, (c,))
+            if ecols.start == 0:
+                y[e] = psum.tile([P, PACK, W * len(E_GROUPS[e])], F32, name="y", bufs=3)
+            product(y[e][:, :, ecols], wd_words, wd_scales[:, :], h_words[k][:, cols], h_scales[k][:, cols])
 
         def residual(c):
-            k, cols = place(S_GROUPS, c)
-            g = S_GROUPS[k]
-            ko, ocols = place(O_GROUPS, c)
-            s, a = divmod(c * W, RES_COLS)
-            nc.vector.tensor_tensor(o32[k][:, :, cols], y[c][:], res_sb[s][:, :, a:a + W], ADD)
-            weave(nc.vector.tensor_copy if c == CHUNKS - 1 else nc.scalar.copy, ob[ko][:, ocols, :], o32[k][:, :, cols])
-            if c == g[-1]:
-                nc.sync.dma_start(out_rows[:, :, g[0] * W:(c + 1) * W], o32[k][:])
+            e, ecols = place(E_GROUPS, (c,))
+            chunks = E_GROUPS[e]
+            if c != chunks[-1]:
+                return
+            k, cols = place(S_GROUPS, chunks)
+            s, a = divmod(chunks[0] * W, RES_COLS)
+            nc.vector.tensor_tensor(o32[k][:, :, cols], y[e][:], res_sb[s][:, :, a:a + W * len(chunks)], ADD)
+            for f in F_GROUPS:
+                if f[-1] in chunks:
+                    kf, fcols = place(S_GROUPS, f)
+                    ko, ocols = place(O_GROUPS, f)
+                    weave(nc.vector.tensor_copy if f[-1] in (7,) else nc.scalar.copy, ob[ko][:, ocols, :], o32[kf][:, :, fcols])
+            if c == S_GROUPS[k][-1]:
+                nc.sync.dma_start(out_rows[:, :, span(S_GROUPS[k])], o32[k][:])
 
         def planes_out(c):
-            k, cols = place(O_GROUPS, c)
+            k, cols = place(O_GROUPS, (c,))
             g = O_GROUPS[k]
             if c == g[-1]:
-                kw, last = place(WORD_STORES, c)
-                quantize(o_words[kw][:, last.stop - len(g) * W:last.stop], o_scales[:, g[0] * W:(c + 1) * W], ob[k][:])
+                kw, wcols = place(WORD_STORES, g)
+                quantize(o_words[kw][:, wcols], o_scales[:, span(g)], ob[k][:])
                 if c == WORD_STORES[kw][-1]:
-                    nc.sync.dma_start(out_words[:, WORD_STORES[kw][0] * W:(c + 1) * W], o_words[kw][:])
+                    nc.sync.dma_start(out_words[:, span(WORD_STORES[kw])], o_words[kw][:])
 
-        stages = ((last_plane, 0), (first_products, 1), (gate, 2), (quantize_h, 3), (second_product, 4), (residual, 5), (planes_out, 7))
-        for step in range(CHUNKS + 7):
+        stages = ((last_plane, 0), (first_products, 1), (gate, 2), (quantize_h, 3), (second_product, 5), (residual, 7), (planes_out, 9))
+        for step in range(CHUNKS + 9):
             if step == 0:
-                for k in range(WD_PARTS):
-                    deal_wd(k)
+                for u, copy in enumerate((nc.scalar.copy, nc.vector.tensor_copy)):
+                    copy(wd_bf[:].rearrange("p (t m) i -> p m i t", t=4)[:, :, :, 2 * u:2 * u + 2],
+                         wd_raw[:].rearrange("p i (m t) -> p m i t", t=4)[:, :, :, 2 * u:2 * u + 2])
             if step == 1:
                 quantize(wd_words[:], wd_scales[:], wd_bf[:])
             for stage, lag in reversed(stages):

from contextlib import ExitStack

import concourse.mybir as mybir

K, R, N, T, J = 512, 512, 512, 2048, 1024
FLOPS = 2 * J * (K * R * 2 + R * N)

F32 = mybir.dt.float32
BF16 = mybir.dt.bfloat16
I32 = mybir.dt.int32
U16 = mybir.dt.uint16
U8 = mybir.dt.uint8
FP8X4 = mybir.dt.float8_e4m3fn_x4
MULT = mybir.AluOpType.mult
ADD = mybir.AluOpType.add
TANH = mybir.ActivationFunctionType.Tanh

P = 128
PACK = 4
W = 128
CHUNKS = J // W
X_GROUPS = ((0,), (1,), (2, 3), (4, 5), (6, 7))
H_GROUPS = ((0, 1), (2, 3), (4, 5), (6, 7))
E_GROUPS = tuple((c,) for c in range(CHUNKS))
F_GROUPS = tuple((c,) for c in range(CHUNKS))
O_GROUPS = ((0, 1, 2, 3), (4, 5), (6,), (7,))
S_GROUPS = ((0, 1), (2, 3), (4, 5), (6, 7))
WORD_STORES = ((0, 1, 2, 3), (4, 5, 6, 7))
RES_COLS = 1024


def span(chunks):
    return slice(chunks[0] * W, (chunks[-1] + 1) * W)


def place(groups, chunks):
    k = [g for g, members in enumerate(groups) if chunks[0] in members][0]
    first = groups[k][0] * W
    return k, slice(chunks[0] * W - first, (chunks[-1] + 1) * W - first)


def tile_list_tanh_resP_kernel(tc, xT, wgt, wg_words, wg_scales, wu_words, wu_scales, wd, res, offs, out_0, out_1, out_2):
    nc = tc.nc
    with ExitStack() as ctx:
        keep = ctx.enter_context(tc.tile_pool(name="keep", bufs=1))
        psum = ctx.enter_context(tc.psum_pool(name="psum", bufs=1))

        wgt_cut = keep.tile([P, W], F32, name="wgt_cut", align_bytes=64)
        nc.sync.dma_start(wgt_cut[:], wgt.rearrange("(a r) (s c) -> r a s c", r=8, c=W)[0])
        x_rows = xT.rearrange("(p i) t -> i p t", i=PACK)
        planes = [keep.tile([P, T], F32, name=f"plane{i}") for i in range(PACK)]
        nc.sync.dma_start(planes[0][:], x_rows[0])
        offsets = keep.tile([P, J // 16], U16, name="offsets")
        nc.sync.dma_start(offsets[:], offs)
        scales_raw = keep.tile([P, R], U8, name="scales_raw")
        nc.vector.memset(scales_raw[:].bitcast(I32), 0)

        def load_scales(first, scales):
            for q in range(4):
                nc.sync.dma_start(scales_raw[32 * q + first:32 * q + first + 4, :].bitcast(I32),
                                  scales[0, 4 * q:4 * q + 4, :].bitcast(I32))

        nc.sync.dma_start(planes[1][:], x_rows[1])
        load_scales(0, wg_scales)
        nc.sync.dma_start(planes[2][:], x_rows[2])
        words_raw = keep.tile([P, 2, R], I32, name="words_raw")
        for k, words in enumerate((wg_words, wu_words)):
            nc.sync.dma_start(words_raw[:, k, :], words[0].rearrange("p r i -> p (r i)").bitcast(I32))
        load_scales(4, wu_scales)
        nc.sync.dma_start(planes[3][:], x_rows[3])
        wd_raw = keep.tile([P, PACK, N], F32, name="wd_raw")
        wd_rows = wd.rearrange("(q i s) n -> i q s n", i=PACK, s=8)
        for i in range(PACK):
            nc.sync.dma_start(wd_raw[:, i, :], wd_rows[i])
        res_rows = res.rearrange("(p t) j -> p t j", t=PACK)
        res_sb = []
        for s in range(J // RES_COLS):
            part = keep.tile([P, PACK, RES_COLS], F32, name=f"res{s}")
            nc.sync.dma_start(part[:], res_rows[:, :, s * RES_COLS:(s + 1) * RES_COLS])
            res_sb.append(part)

        warm = keep.tile([P, 1], F32, name="warm")
        nc.vector.memset(warm[:], 0.0)
        nc.scalar.activation(warm[:], warm[:], TANH)

        wgt_turned = keep.tile([P, W], F32, name="wgt_turned", align_bytes=64)
        nc.vector.transpose(wgt_turned[:], wgt_cut[:])
        by_head = wgt_turned[:].rearrange("p (b h d s) -> p s b h d", b=4, h=2, d=2)
        wgt_full = keep.tile([P, J], F32, name="wgt_full", align_bytes=64)
        pieces = ((0, 2, nc.vector.tensor_copy), (2, 4, nc.vector.tensor_copy), (4, 8, nc.scalar.copy))
        spread = [keep.tile([P, (b - a) * W], F32, name=f"wgt_spread{a}", align_bytes=64) for a, b, copy in pieces]
        for tile, (a, b, copy) in zip(spread, pieces):
            copy(tile[:].rearrange("p (s b h r) -> p s b h r", b=4, h=2, r=16),
                 by_head[:, a:b, :, :, 0:1].to_broadcast([P, b - a, 4, 2, 16]))
        for tile, (a, b, copy) in zip(spread, pieces):
            nc.vector.transpose(wgt_full[:, a * W:b * W], tile[:])

        def gather(out, i, cols):
            nc.vector.tensor_tensor(out, planes[i][:].indirect(offsets[:, cols.start // 16:cols.stop // 16]),
                                    wgt_full[:, cols], MULT)

        def weave(engine_copy, dst, src):
            engine_copy(dst.rearrange("p (c i) t -> p c t i", i=2), src.rearrange("p t (c i) -> p c t i", i=2))

        def quantize(words, scales, src):
            nc.vector.quantize_mx(out=words.bitcast(FP8X4), scales=scales, in_=src.rearrange("p j t -> p (j t)"))

        def product(out, words, scales, rhs, rhs_scale):
            for t in range(PACK):
                cols = slice(t * P, (t + 1) * P)
                nc.tensor.matmul_mx(out=out[:, t, :], lhsT=words[:, cols].bitcast(FP8X4), lhsT_scale=scales[:, cols],
                                    rhs=rhs.bitcast(FP8X4), rhs_scale=rhs_scale, start=True, stop=True)

        def group_tiles(groups, name, shape_of, dtype):
            return [keep.tile(shape_of(W * len(g)), dtype, name=f"{name}{k}", align_bytes=64) for k, g in enumerate(groups)]

        g01 = keep.tile([P, 2, J], F32, name="g01")
        gather(g01[:, 0, :J // 2], 0, slice(0, J // 2))
        gather(g01[:, 0, J // 2:], 0, slice(J // 2, J))
        gather(g01[:, 1, :], 1, slice(0, J))
        g23 = group_tiles(X_GROUPS, "g23_", lambda w: [P, 2, w], F32)
        xb = group_tiles(X_GROUPS, "xb", lambda w: [P, w, PACK], BF16)
        for k, g in enumerate(X_GROUPS):
            nc.scalar.copy(xb[k][:, :, 0:2], g01[:, :, span(g)].rearrange("p t j -> p j t"))
        for k, g in enumerate(X_GROUPS):
            gather(g23[k][:, 0, :], 2, span(g))

        w1_words = keep.tile([P, 2, R], I32, name="w1_words", align_bytes=64)
        w1_scales = keep.tile([P, R], U8, name="w1_scales", align_bytes=64)
        nc.vector.tensor_copy(w1_words[:].rearrange("p k (t q s) -> p k q t s", t=4, s=8),
                              words_raw[:].rearrange("p k (q t s) -> p k q t s", t=4, s=8))
        nc.vector.tensor_copy(w1_scales[:].bitcast(I32).rearrange("p (t q s) -> p t q s", t=4, s=2),
                              scales_raw[:].bitcast(I32).rearrange("p (q t s) -> p t q s", t=4, s=2))

        wd_bf = keep.tile([P, N, PACK], BF16, name="wd_bf", align_bytes=64)
        wd_words = keep.tile([P, N], I32, name="wd_words", align_bytes=64)
        wd_scales = keep.tile([P, N], U8, name="wd_scales", align_bytes=64)

        out_rows = out_0.rearrange("(p t) j -> p t j", t=PACK)
        out_words = out_1[0].rearrange("p j i -> p (j i)").bitcast(I32)
        o_scales = keep.tile([P, J], U8, name="o_scales", align_bytes=64)
        x_words = group_tiles(X_GROUPS, "x_words", lambda w: [P, w], I32)
        x_scales = group_tiles(X_GROUPS, "x_scales", lambda w: [P, w], U8)
        hb = group_tiles(H_GROUPS, "hb", lambda w: [P, w, PACK], BF16)
        h_words = group_tiles(H_GROUPS, "h_words", lambda w: [P, w], I32)
        h_scales = group_tiles(H_GROUPS, "h_scales", lambda w: [P, w], U8)
        o32 = group_tiles(S_GROUPS, "o32", lambda w: [P, PACK, w], F32)
        ob = group_tiles(O_GROUPS, "ob", lambda w: [P, w, PACK], BF16)
        o_words = group_tiles(WORD_STORES, "o_words", lambda w: [P, w], I32)
        ub, th, y = {}, {}, {}

        def last_plane(c):
            k, cols = place(X_GROUPS, (c,))
            if cols.start == 0:
                gather(g23[k][:, 1, :], 3, span(X_GROUPS[k]))
                nc.scalar.copy(xb[k][:, :, 2:4], g23[k][:].rearrange("p t j -> p j t"))

        def first_products(c):
            k, cols = place(X_GROUPS, (c,))
            if cols.start == 0:
                quantize(x_words[k][:], x_scales[k][:], xb[k][:])
            ga = psum.tile([P, PACK, W], F32, name="ga", bufs=2)
            ub[c] = psum.tile([P, PACK, W], F32, name="ub", bufs=3)
            product(ub[c], w1_words[:, 1, :], w1_scales[4:, :], x_words[k][:, cols], x_scales[k][:, cols])
            product(ga, w1_words[:, 0, :], w1_scales[:, :], x_words[k][:, cols], x_scales[k][:, cols])
            th[c] = keep.tile([P, W, PACK], F32, name=f"th{c}")
            nc.scalar.activation(th[c][:], ga[:].rearrange("p t j -> p j t"), TANH)

        def gate(c):
            k, cols = place(H_GROUPS, (c,))
            nc.vector.tensor_tensor(hb[k][:, cols, :], ub[c][:].rearrange("p t j -> p j t"), th[c][:], MULT)

        def quantize_h(c):
            k, cols = place(H_GROUPS, (c,))
            if c == H_GROUPS[k][-1]:
                quantize(h_words[k][:], h_scales[k][:], hb[k][:])

        def second_product(c):
            k, cols = place(H_GROUPS, (c,))
            e, ecols = place(E_GROUPS, (c,))
            if ecols.start == 0:
                y[e] = psum.tile([P, PACK, W * len(E_GROUPS[e])], F32, name="y", bufs=3)
            product(y[e][:, :, ecols], wd_words, wd_scales[:, :], h_words[k][:, cols], h_scales[k][:, cols])

        def residual(c):
            e, ecols = place(E_GROUPS, (c,))
            chunks = E_GROUPS[e]
            if c != chunks[-1]:
                return
            k, cols = place(S_GROUPS, chunks)
            s, a = divmod(chunks[0] * W, RES_COLS)
            nc.vector.tensor_tensor(o32[k][:, :, cols], y[e][:], res_sb[s][:, :, a:a + W * len(chunks)], ADD)
            for f in F_GROUPS:
                if f[-1] in chunks:
                    kf, fcols = place(S_GROUPS, f)
                    ko, ocols = place(O_GROUPS, f)
                    weave(nc.vector.tensor_copy if f[-1] in (7,) else nc.scalar.copy, ob[ko][:, ocols, :], o32[kf][:, :, fcols])
            if c == S_GROUPS[k][-1]:
                nc.sync.dma_start(out_rows[:, :, span(S_GROUPS[k])], o32[k][:])

        def planes_out(c):
            k, cols = place(O_GROUPS, (c,))
            g = O_GROUPS[k]
            if c == g[-1]:
                kw, wcols = place(WORD_STORES, g)
                quantize(o_words[kw][:, wcols], o_scales[:, span(g)], ob[k][:])
                if c == WORD_STORES[kw][-1]:
                    nc.sync.dma_start(out_words[:, span(WORD_STORES[kw])], o_words[kw][:])

        stages = ((last_plane, 0), (first_products, 1), (gate, 2), (quantize_h, 3), (second_product, 5), (residual, 7), (planes_out, 9))
        for step in range(CHUNKS + 9):
            if step == 0:
                for u, copy in enumerate((nc.scalar.copy, nc.vector.tensor_copy)):
                    copy(wd_bf[:].rearrange("p (t m) i -> p m i t", t=4)[:, :, :, 2 * u:2 * u + 2],
                         wd_raw[:].rearrange("p i (m t) -> p m i t", t=4)[:, :, :, 2 * u:2 * u + 2])
            if step == 1:
                quantize(wd_words[:], wd_scales[:], wd_bf[:])
            for stage, lag in reversed(stages):
                if 0 <= step - lag < CHUNKS:
                    stage(step - lag)

        for q in range(4):
            queue = nc.scalar if q % 2 else nc.sync
            queue.dma_start(out_2[0, 4 * q:4 * q + 4, :].bitcast(I32), o_scales[32 * q:32 * q + 4, :].bitcast(I32))
